import numpy as np, ml_dtypes
CORES = [52,53,54,55,60,61,62,63]
N = 8
def setup_inputs(rng):
    return {"x": rng.standard_normal((N, 128, 4), dtype=np.float32).astype(ml_dtypes.bfloat16)}
def reference(x):
    s = x.max(axis=0)
    return {"y": np.broadcast_to(s, (N,) + s.shape)}

@@ -1,0 +1,57 @@
+import concourse.bass as bass
+
+W = 4
+SCRATCH = {
+    "mine": ("sbuf", [128, W], "bfloat16"),
+    "gather": ("sbuf", [128, 5 * W], "bfloat16"),
+    "res": ("sbuf", [128, W], "bfloat16"),
+}
+SEMAPHORES = ["local", "sent", "arrived", "partial", "done"]
+
+ON_CHIP = 0xFFFF
+OFF_CHIP = 0x00FF
+HELPER_CORE = 2
+
+
+def slot(T, k):
+    return T.gather[:, k * W:(k + 1) * W]
+
+
+def dst_id(topo, c):
+    rid, pid, se = topo.addr(c)
+    return bass.DstId(rid=rid, pnc=pid)
+
+
+def rank_program(g, core, T, topo):
+    chips = sorted(set(topo.chip(c) for c in T.cores))
+    helpers = {ch: ch * 8 + HELPER_CORE for ch in chips}
+    ch = topo.chip(core)
+    rank = T.rank_of(core)
+
+    if rank is not None:
+        members = [c for c in T.cores if topo.chip(c) == ch]
+        k = members.index(core)
+        g.dma_start(T.mine[:], T.x[:]).then_inc(T.sem.local, 16)
+        g.wait_ge(T.sem.local, 16)
+        rid, pid, se = topo.addr(helpers[ch])
+        g.remote_dma(slot(T, k), T.mine[:], T.sem.arrived, T.sem.sent, pid, rid, ON_CHIP)
+        g.wait_ge(T.sem.done, 16)
+        g.dma_start(T.y[:], T.res[:]).then_inc(T.sem.local, 16)
+        g.wait_ge(T.sem.sent, 16)
+        g.wait_ge(T.sem.local, 32)
+        return
+
+    if ch in helpers and helpers[ch] == core:
+        members = [c for c in T.cores if topo.chip(c) == ch]
+        other = [helpers[o] for o in chips if o != ch][0]
+        n = len(members)
+        g.wait_ge(T.sem.arrived, 16 * n)
+        g.remote_dma_fused([bass.RemoteDMATransfer(
+            dst_ids=[dst_id(topo, other)], dma_engine_mask=OFF_CHIP, remote_sem=T.sem.partial,
+            srcs=[slot(T, j) for j in range(n)], dsts=[slot(T, n)], alu_op=2)], local_sem=T.sem.sent)
+        g.wait_ge(T.sem.partial, 8)
+        g.remote_dma_fused([bass.RemoteDMATransfer(
+            dst_ids=[dst_id(topo, c) for c in members], dma_engine_mask=ON_CHIP, remote_sem=T.sem.done,
+            srcs=[slot(T, j) for j in range(n + 1)], dsts=[T.res[:] for c in members], alu_op=2)],
+            local_sem=T.sem.sent)
+        g.wait_ge(T.sem.sent, 8 + 16)

@@ -2,9 +2,9 @@ import concourse.bass as bass
 
 W = 4
 SCRATCH = {
-    "mine": ("sbuf", [128, W], "bfloat16"),
-    "gather": ("sbuf", [128, 5 * W], "bfloat16"),
-    "res": ("sbuf", [128, W], "bfloat16"),
+    "mine": ("dram", [128, W], "bfloat16"),
+    "gather": ("dram", [5, 128, W], "bfloat16"),
+    "res": ("dram", [128, W], "bfloat16"),
 }
 SEMAPHORES = ["local", "sent", "arrived", "partial", "done"]
 
@@ -14,7 +14,7 @@ HELPER_CORE = 2
 
 
 def slot(T, k):
-    return T.gather[:, k * W:(k + 1) * W]
+    return T.gather[k]
 
 
 def dst_id(topo, c):

@@ -10,11 +10,6 @@ SEMAPHORES = ["local", "sent", "arrived", "partial", "done"]
 
 ON_CHIP = 0xFFFF
 OFF_CHIP = 0x00FF
-HELPER_CORE = 2
-
-
-def slot(T, k):
-    return T.gather[k]
 
 
 def dst_id(topo, c):
@@ -23,35 +18,39 @@ def dst_id(topo, c):
 
 
 def rank_program(g, core, T, topo):
-    chips = sorted(set(topo.chip(c) for c in T.cores))
-    helpers = {ch: ch * 8 + HELPER_CORE for ch in chips}
-    ch = topo.chip(core)
-    rank = T.rank_of(core)
-
-    if rank is not None:
-        members = [c for c in T.cores if topo.chip(c) == ch]
-        k = members.index(core)
-        g.dma_start(T.mine[:], T.x[:]).then_inc(T.sem.local, 16)
-        g.wait_ge(T.sem.local, 16)
-        rid, pid, se = topo.addr(helpers[ch])
-        g.remote_dma(slot(T, k), T.mine[:], T.sem.arrived, T.sem.sent, pid, rid, ON_CHIP)
-        g.wait_ge(T.sem.done, 16)
-        g.dma_start(T.y[:], T.res[:]).then_inc(T.sem.local, 16)
-        g.wait_ge(T.sem.sent, 16)
-        g.wait_ge(T.sem.local, 32)
+    if T.rank_of(core) is None:
         return
+    ch = topo.chip(core)
+    members = [c for c in T.cores if topo.chip(c) == ch]
+    n = len(members)
+    k = members.index(core)
+    folders = members[2:]
+    plain = members[:2]
 
-    if ch in helpers and helpers[ch] == core:
-        members = [c for c in T.cores if topo.chip(c) == ch]
-        other = [helpers[o] for o in chips if o != ch][0]
-        n = len(members)
-        g.wait_ge(T.sem.arrived, 16 * n)
+    g.dma_start(T.mine[:], T.x[:]).then_inc(T.sem.local, 16)
+    g.wait_ge(T.sem.local, 16)
+    to = [f for f in folders if f != core]
+    g.remote_dma_fused([bass.RemoteDMATransfer(
+        dst_ids=[dst_id(topo, f) for f in to], dma_engine_mask=ON_CHIP, remote_sem=T.sem.arrived,
+        srcs=[T.mine[:]], dsts=[T.gather[k] for f in to], alu_op=0)], local_sem=T.sem.sent)
+    sent = 16
+
+    if core in folders:
+        i = folders.index(core)
+        counterpart = core ^ 8
+        tiles = [T.mine[:] if j == k else T.gather[j] for j in range(n)]
+        g.wait_ge(T.sem.arrived, 16 * (n - 1))
         g.remote_dma_fused([bass.RemoteDMATransfer(
-            dst_ids=[dst_id(topo, other)], dma_engine_mask=OFF_CHIP, remote_sem=T.sem.partial,
-            srcs=[slot(T, j) for j in range(n)], dsts=[slot(T, n)], alu_op=2)], local_sem=T.sem.sent)
+            dst_ids=[dst_id(topo, counterpart)], dma_engine_mask=OFF_CHIP, remote_sem=T.sem.partial,
+            srcs=tiles, dsts=[T.gather[n]], alu_op=2)], local_sem=T.sem.sent)
         g.wait_ge(T.sem.partial, 8)
+        serve = [plain[i], folders[1 - i]]
         g.remote_dma_fused([bass.RemoteDMATransfer(
-            dst_ids=[dst_id(topo, c) for c in members], dma_engine_mask=ON_CHIP, remote_sem=T.sem.done,
-            srcs=[slot(T, j) for j in range(n + 1)], dsts=[T.res[:] for c in members], alu_op=2)],
-            local_sem=T.sem.sent)
-        g.wait_ge(T.sem.sent, 8 + 16)
+            dst_ids=[dst_id(topo, c) for c in serve], dma_engine_mask=ON_CHIP, remote_sem=T.sem.done,
+            srcs=tiles + [T.gather[n]], dsts=[T.res[:] for c in serve], alu_op=2)], local_sem=T.sem.sent)
+        sent += 8 + 16
+
+    g.wait_ge(T.sem.done, 16)
+    g.dma_start(T.y[:], T.res[:]).then_inc(T.sem.local, 16)
+    g.wait_ge(T.sem.sent, sent)
+    g.wait_ge(T.sem.local, 32)

@@ -24,31 +24,32 @@ def rank_program(g, core, T, topo):
     members = [c for c in T.cores if topo.chip(c) == ch]
     n = len(members)
     k = members.index(core)
-    folders = members[2:]
-    plain = members[:2]
+    C, D, A, B = members
+    mate = 8 * ((ch ^ 1) - ch)
 
     g.dma_start(T.mine[:], T.x[:]).then_inc(T.sem.local, 16)
     g.wait_ge(T.sem.local, 16)
-    to = [f for f in folders if f != core]
+    to = [f for f in (A, B, C) if f != core]
     g.remote_dma_fused([bass.RemoteDMATransfer(
         dst_ids=[dst_id(topo, f) for f in to], dma_engine_mask=ON_CHIP, remote_sem=T.sem.arrived,
         srcs=[T.mine[:]], dsts=[T.gather[k] for f in to], alu_op=0)], local_sem=T.sem.sent)
     sent = 16
 
-    if core in folders:
-        i = folders.index(core)
-        counterpart = core ^ 8
+    if core != D:
         tiles = [T.mine[:] if j == k else T.gather[j] for j in range(n)]
         g.wait_ge(T.sem.arrived, 16 * (n - 1))
-        g.remote_dma_fused([bass.RemoteDMATransfer(
-            dst_ids=[dst_id(topo, counterpart)], dma_engine_mask=OFF_CHIP, remote_sem=T.sem.partial,
-            srcs=tiles, dsts=[T.gather[n]], alu_op=2)], local_sem=T.sem.sent)
+        across = {A: [A + mate, C + mate], B: [B + mate], C: []}[core]
+        if across:
+            g.remote_dma_fused([bass.RemoteDMATransfer(
+                dst_ids=[dst_id(topo, c) for c in across], dma_engine_mask=OFF_CHIP, remote_sem=T.sem.partial,
+                srcs=tiles, dsts=[T.gather[n] for c in across], alu_op=2)], local_sem=T.sem.sent)
+            sent += 8
         g.wait_ge(T.sem.partial, 8)
-        serve = [plain[i], folders[1 - i]]
+        serve = {A: [C, B], B: [A], C: [D]}[core]
         g.remote_dma_fused([bass.RemoteDMATransfer(
             dst_ids=[dst_id(topo, c) for c in serve], dma_engine_mask=ON_CHIP, remote_sem=T.sem.done,
             srcs=tiles + [T.gather[n]], dsts=[T.res[:] for c in serve], alu_op=2)], local_sem=T.sem.sent)
-        sent += 8 + 16
+        sent += 16
 
     g.wait_ge(T.sem.done, 16)
     g.dma_start(T.y[:], T.res[:]).then_inc(T.sem.local, 16)

import concourse.bass as bass

W = 4
SCRATCH = {
    "mine": ("dram", [128, W], "bfloat16"),
    "gather": ("dram", [5, 128, W], "bfloat16"),
    "res": ("dram", [128, W], "bfloat16"),
}
SEMAPHORES = ["local", "sent", "arrived", "partial", "done"]

ON_CHIP = 0xFFFF
OFF_CHIP = 0x00FF


def dst_id(topo, c):
    rid, pid, se = topo.addr(c)
    return bass.DstId(rid=rid, pnc=pid)


def rank_program(g, core, T, topo):
    if T.rank_of(core) is None:
        return
    ch = topo.chip(core)
    members = [c for c in T.cores if topo.chip(c) == ch]
    n = len(members)
    k = members.index(core)
    C, D, A, B = members
    mate = 8 * ((ch ^ 1) - ch)

    g.dma_start(T.mine[:], T.x[:]).then_inc(T.sem.local, 16)
    g.wait_ge(T.sem.local, 16)
    to = [f for f in (A, B, C) if f != core]
    g.remote_dma_fused([bass.RemoteDMATransfer(
        dst_ids=[dst_id(topo, f) for f in to], dma_engine_mask=ON_CHIP, remote_sem=T.sem.arrived,
        srcs=[T.mine[:]], dsts=[T.gather[k] for f in to], alu_op=0)], local_sem=T.sem.sent)
    sent = 16

    if core != D:
        tiles = [T.mine[:] if j == k else T.gather[j] for j in range(n)]
        g.wait_ge(T.sem.arrived, 16 * (n - 1))
        across = {A: [A + mate, C + mate], B: [B + mate], C: []}[core]
        if across:
            g.remote_dma_fused([bass.RemoteDMATransfer(
                dst_ids=[dst_id(topo, c) for c in across], dma_engine_mask=OFF_CHIP, remote_sem=T.sem.partial,
                srcs=tiles, dsts=[T.gather[n] for c in across], alu_op=2)], local_sem=T.sem.sent)
            sent += 8
        g.wait_ge(T.sem.partial, 8)
        serve = {A: [C, B], B: [A], C: [D]}[core]
        g.remote_dma_fused([bass.RemoteDMATransfer(
            dst_ids=[dst_id(topo, c) for c in serve], dma_engine_mask=ON_CHIP, remote_sem=T.sem.done,
            srcs=tiles + [T.gather[n]], dsts=[T.res[:] for c in serve], alu_op=2)], local_sem=T.sem.sent)
        sent += 16

    g.wait_ge(T.sem.done, 16)
    g.dma_start(T.y[:], T.res[:]).then_inc(T.sem.local, 16)
    g.wait_ge(T.sem.sent, sent)
    g.wait_ge(T.sem.local, 32)
